import numpy as np
import ml_dtypes


def mxq(x, axis, fmt="e4m3"):
    dtype, down = {"e4m3": (ml_dtypes.float8_e4m3fn, 7), "e5m2": (ml_dtypes.float8_e5m2, 14)}[fmt]
    v = np.moveaxis(np.asarray(x, np.float32).astype(ml_dtypes.bfloat16).astype(np.float64), axis, -1)
    blocks = v.reshape(v.shape[:-1] + (-1, 32))
    amax = np.abs(blocks).max(-1, keepdims=True)
    byte = np.maximum(np.where(amax > 0, np.frexp(amax)[1] - 1 + 127, 0) - down, 1)
    scale = np.exp2(byte - 127.0)
    codes = (blocks / scale).astype(np.float32).astype(dtype).astype(np.float64)
    return np.moveaxis((codes * scale).reshape(v.shape), -1, axis)


WIDE = False


def mx_kscale(k):
    if not WIDE:
        return np.ones(k)
    levels = np.array([10, -10, 5, -5, 0])
    if k % 512:
        return np.exp2(np.random.permutation(np.resize(levels, k // 32))).repeat(32)
    a = np.empty((k // 512, 16))
    for p in range(k // 512):
        a[p, :8] = np.random.permutation(np.resize(levels, 8))
        for g in range(8):
            far = levels[np.abs(levels - a[p, g]) >= 10]
            a[p, g + 8] = far[np.random.randint(len(far))]
    return np.exp2(a.ravel()).repeat(32)


def f64(x):
    return np.asarray(x).astype(np.float64)


def striped(idx):
    return np.tile(np.asarray(idx).reshape(-1, 16).T, (8, 1)).astype(np.uint16)


def unstriped(offs):
    return offs[:16].T.reshape(-1).astype(np.int64)


def striped8(idx):
    return np.asarray(idx).reshape(8, -1, 16).transpose(0, 2, 1).reshape(128, -1).astype(np.uint16)


def unstriped8(offs):
    return offs.reshape(8, 16, -1).transpose(0, 2, 1).reshape(8, -1).astype(np.int64)


def pick8(x, idx, run):
    r = np.arange(len(x))
    return x[r[:, None], idx[r % (8 * run) // run]]


E2M1 = np.array([0.0, 0.5, 1.0, 1.5, 2.0, 3.0, 4.0, 6.0, -0.0, -0.5, -1.0, -1.5, -2.0, -3.0, -4.0, -6.0])


def pack_weight(w, fmt):
    k, n = w.shape
    w = f64(np.asarray(w, np.float32).astype(ml_dtypes.bfloat16)).reshape(k // 32, 32, n)
    amax = np.abs(w).max(1)
    if fmt == "e4m3":
        byte = np.frexp(amax)[1] - 1 + 127 - 7
    else:
        mant, ex = np.frexp(amax / 6.0)
        byte = np.where(mant > 0.5, ex, ex - 1) + 127
    byte = np.clip(np.where(amax > 0, byte, 1), 1, 254)
    scaled = (w * np.exp2(127.0 - byte)[:, None, :]).reshape(k, n).astype(np.float32)
    by_word = np.ascontiguousarray(scaled.reshape(k // 512, 128, 4, n).transpose(0, 1, 3, 2))
    if fmt == "e4m3":
        words = by_word.astype(ml_dtypes.float8_e4m3fn).view(np.uint8)
    else:
        c = by_word.astype(ml_dtypes.float4_e2m1fn).view(np.uint8) & 0xF
        words = (c[..., 0::2] | (c[..., 1::2] << 4)).reshape(k // 512, 128, 2 * n)
    return np.ascontiguousarray(words), np.ascontiguousarray(byte.astype(np.uint8).reshape(k // 512, 16, n))


def unpack_weight(words, scales, fmt):
    g, _, n = scales.shape
    words = np.ascontiguousarray(words).reshape(g, 128, n, -1)
    if fmt == "e4m3":
        vals = words.view(ml_dtypes.float8_e4m3fn).astype(np.float64)
    else:
        nib = np.empty((g, 128, n, 4), np.uint8)
        nib[..., 0::2] = words & 0xF
        nib[..., 1::2] = words >> 4
        vals = E2M1[nib]
    vals = vals * np.repeat(np.exp2(scales.astype(np.float64) - 127.0), 8, axis=1)[..., None]
    return vals.transpose(0, 1, 3, 2).reshape(g * 512, n)


K, J, R, T, U, Z, M, O, D, N = 512, 256, 512, 512, 512, 512, 1024, 128, 512, 256


def setup_inputs():
    n = np.random.standard_normal
    idx = np.stack([np.random.permutation(T)[:J] for _ in range(8)])
    idx2 = np.stack([np.random.permutation(U)[:J] for _ in range(8)])
    idx3 = np.stack([np.random.permutation(U)[:J] for _ in range(8)])
    idx4 = np.random.permutation(M)[:J]
    idx5 = np.stack([np.random.permutation(J)[:O] for _ in range(8)])
    idx6 = np.stack([np.random.permutation(D)[:O] for _ in range(8)])
    idx7 = np.stack([np.random.permutation(D)[:O] for _ in range(8)])
    fk = mx_kscale(K)
    fr = mx_kscale(R)
    fz = mx_kscale(Z)
    wp = pack_weight(n((K, R)) * 1 / np.sqrt(K) / fk[:, None] * fr, "e2m1")
    xop = pack_weight(n((Z, M)) / fz[:, None], "e2m1")
    w2p = pack_weight(n((Z, R)) * 1 / np.sqrt(Z) * fz[:, None] * fr, "e4m3")
    wbp = pack_weight(n((R, N)) * 1 / np.sqrt(R) / fr[:, None], "e4m3")
    return {
        "ta": (np.random.randint(-7, 8, (K, T)).astype(np.float64)).astype(np.float32),
        "ga": ((np.random.randint(8, 25, (K, 1)) / 64.0) * fk[:, None]).astype(np.float32),
        "gb": (np.random.uniform(0.5, 1.6, (K, 1))).astype(np.float32),
        "w_words": wp[0],
        "w_scales": wp[1],
        "xo_words": xop[0],
        "xo_scales": xop[1],
        "w2_words": w2p[0],
        "w2_scales": w2p[1],
        "tl": (np.random.randint(-7, 8, (R, D)).astype(np.float64)).astype(np.float32),
        "sa": (np.random.uniform(0.5, 1.6, (R, 1))).astype(np.float32),
        "sl": ((np.random.randint(6, 19, (R, 1)) / 64.0) * fr[:, None]).astype(np.float32),
        "sm": ((np.random.randint(4, 15, (R, 1)) / 64.0) * fr[:, None]).astype(np.float32),
        "wb_words": wbp[0],
        "wb_scales": wbp[1],
        "offs": striped8(idx),
        "offs2": striped8(idx2),
        "offs3": striped8(idx3),
        "offs4": striped(idx4),
        "offs5": striped8(idx5),
        "offs6": striped8(idx6),
        "offs7": striped8(idx7),
    }


def reference(ta, ga, gb, w_words, w_scales, xo_words, xo_scales, w2_words, w2_scales, tl, sa, sl, sm, wb_words, wb_scales, offs, offs2, offs3, offs4, offs5, offs6, offs7):
    idx = unstriped8(offs)
    idx2 = unstriped8(offs2)
    idx3 = unstriped8(offs3)
    idx4 = unstriped(offs4)
    idx5 = unstriped8(offs5)
    idx6 = unstriped8(offs6)
    idx7 = unstriped8(offs7)
    wu = unpack_weight(w_words, w_scales, "e2m1")
    xou = unpack_weight(xo_words, xo_scales, "e2m1")
    w2u = unpack_weight(w2_words, w2_scales, "e4m3")
    wbu = unpack_weight(wb_words, wb_scales, "e4m3")
    xcd = pick8(f64(ta), idx, 64) * f64(ga)
    xcp = np.zeros((K, U))
    xcp[np.arange(K)[:, None], idx2[np.arange(K) % 512 // 64]] = xcd
    xc = pick8(xcp, idx3, 64) * f64(gb)
    xcq = mxq(xc, 0, "e4m3")
    xoidx4g = xou[:, idx4]
    a = wu.T @ xcq + w2u.T @ xoidx4g
    hid = np.maximum(np.minimum(pick8(a, idx5, 64) * f64(sa), pick8(f64(tl), idx6, 64) * f64(sl)), pick8(f64(tl), idx7, 64) * f64(sm))
    hidq = mxq(hid, 0, "e4m3")
    y = wbu.T @ hidq
    return y

@@ -1,0 +1,176 @@
+from contextlib import ExitStack
+
+import concourse.mybir as mybir
+
+K, J, R, T, U, Z, M, O, D, N = 512, 256, 512, 512, 512, 512, 1024, 128, 512, 256
+FLOPS = 2 * (K * R * J + Z * R * J + R * N * O)
+
+F32 = mybir.dt.float32
+BF16 = mybir.dt.bfloat16
+I32 = mybir.dt.int32
+U32 = mybir.dt.uint32
+U16 = mybir.dt.uint16
+U8 = mybir.dt.uint8
+FP8X4 = mybir.dt.float8_e4m3fn_x4
+FP4X4 = mybir.dt.float4_e2m1fn_x4
+COPY = mybir.ActivationFunctionType.Copy
+ALU = mybir.AluOpType
+
+P = 128
+PACK = 4
+QUADS = 4
+HALF = J // 2
+
+
+def tile_picked_codepage_plain_bank_codedbounds_one_plain_kernel(
+    tc, ta, ga, gb, w_words, w_scales, xo_words, xo_scales, w2_words, w2_scales, tl, sa, sl, sm,
+    wb_words, wb_scales, offs, offs2, offs3, offs4, offs5, offs6, offs7, out,
+):
+    nc = tc.nc
+    with ExitStack() as ctx:
+        keep = ctx.enter_context(tc.tile_pool(name="keep", bufs=1))
+        psum = ctx.enter_context(tc.psum_pool(name="psum", bufs=1))
+
+        def tile(shape, dtype, name, tag=None):
+            return keep.tile(shape, dtype, name=name, tag=tag or name, align_bytes=64)
+
+        def load_list(src, name):
+            dst = tile(list(src.shape), U16, name)
+            nc.sync.dma_start(dst[:], src)
+            return dst
+
+        def load_column(queue, src, name):
+            dst = tile([P, PACK], F32, name)
+            queue.dma_start(dst[:], src.rearrange("(p t) o -> p (t o)", t=PACK))
+            return dst
+
+        def load_rows(src, t, name):
+            dst = tile([P, src.shape[1]], F32, name)
+            nc.sync.dma_start(dst[:], src.rearrange("(p t) c -> t p c", t=PACK)[t])
+            return dst
+
+        def load_scales(queue, dst, src):
+            for q in range(QUADS):
+                queue.dma_start(dst[32 * q : 32 * q + 4, :].bitcast(I32), src[0, 4 * q : 4 * q + 4, :].bitcast(I32))
+
+        xo_s = tile([P, M], U8, "xo_s")
+        ws_raw = tile([P, 2 * R], U8, "ws_raw")
+        wb_s = tile([P, N], U8, "wb_s")
+        for plane in (wb_s, xo_s, ws_raw):
+            nc.vector.memset(plane[:].bitcast(I32), 0)
+        page = [tile([P, U], F32, f"page{t}") for t in range(PACK)]
+        for t in range(PACK):
+            nc.vector.memset(page[t][:], 0.0)
+
+        ta_rows = [load_rows(ta, 0, "ta0")]
+        ga_c = load_column(nc.scalar, ga, "ga")
+        l1 = load_list(offs, "l1")
+        l2 = load_list(offs2, "l2")
+        sl_c = load_column(nc.gpsimd, sl, "sl")
+        sm_c = load_column(nc.gpsimd, sm, "sm")
+        gb_c = load_column(nc.gpsimd, gb, "gb")
+        sa_c = load_column(nc.gpsimd, sa, "sa")
+        load_scales(nc.gpsimd, wb_s, wb_scales)
+        for t in range(1, 3):
+            ta_rows.append(load_rows(ta, t, f"ta{t}"))
+        w_raw = tile([P, R], U16, "w_raw")
+        nc.sync.dma_start(w_raw[:].bitcast(I32), w_words[0].bitcast(I32))
+        w2_raw = tile([P, R], U32, "w2_raw")
+        nc.sync.dma_start(w2_raw[:].bitcast(I32), w2_words[0].rearrange("p c r -> p (c r)").bitcast(I32))
+        ta_rows.append(load_rows(ta, 3, "ta3"))
+        l6 = load_list(offs6, "l6")
+        l7 = load_list(offs7, "l7")
+        l3 = load_list(offs3, "l3")
+        tl_rows = [load_rows(tl, t, f"tl{t}") for t in range(2)]
+        xo_w = tile([P, M], U16, "xo_w")
+        nc.sync.dma_start(xo_w[:].bitcast(I32), xo_words[0].bitcast(I32))
+        l4 = load_list(offs4, "l4")
+        load_scales(nc.sync, xo_s, xo_scales)
+        load_scales(nc.sync, ws_raw[:, R:], w2_scales)
+        load_scales(nc.sync, ws_raw[:, :R], w_scales)
+        tl_rows = tl_rows + [load_rows(tl, t, f"tl{t}") for t in range(2, PACK)]
+        l5 = load_list(offs5, "l5")
+        wb_w = tile([P, N], U32, "wb_w")
+        nc.sync.dma_start(wb_w[:].bitcast(I32), wb_words[0].rearrange("p c r -> p (c r)").bitcast(I32))
+
+        for t in range(PACK):
+            xcd = tile([P, J], F32, f"xcd{t}")
+            nc.scalar.activation(xcd[:], ta_rows[t][:].indirect(l1[:]), COPY, scale=ga_c[:, t : t + 1])
+            nc.vector.tensor_copy(page[t][:].indirect(l2[:]), xcd[:])
+
+        w_d = tile([P, R], U16, "w_d")
+        w2_d = tile([P, R], U32, "w2_d")
+        for dealt, raw in ((w_d, w_raw), (w2_d, w2_raw)):
+            nc.scalar.copy(dealt[:].rearrange("p (t m) -> p m t", t=PACK), raw[:].rearrange("p (m t) -> p m t", t=PACK))
+
+        upper = tile([P, PACK, O], F32, "upper")
+        lower = tile([P, PACK, O], F32, "lower")
+
+        def fetch_bounds(t):
+            nc.scalar.activation(upper[:, t, :], tl_rows[t][:].indirect(l6[:]), COPY, scale=sl_c[:, t : t + 1])
+            nc.scalar.activation(lower[:, t, :], tl_rows[t][:].indirect(l7[:]), COPY, scale=sm_c[:, t : t + 1])
+
+        for t in range(2):
+            fetch_bounds(t)
+        xb = tile([P, PACK, J], BF16, "xb", tag="tl1")
+        for t in range(PACK):
+            nc.scalar.activation(xb[:, t, :], page[t][:].indirect(l3[:]), COPY, scale=gb_c[:, t : t + 1])
+        for t in range(2, PACK):
+            fetch_bounds(t)
+
+        xg_w = tile([P, J], U16, "xg_w")
+        xg_s = tile([P, J], U8, "xg_s")
+        nc.vector.tensor_copy(xg_w[:], xo_w[:].indirect(l4[:]))
+        nc.vector.tensor_copy(xg_s[:], xo_s[:].indirect(l4[:]))
+
+        ws = tile([P, 2, R], U8, "ws")
+        nc.vector.tensor_copy(
+            ws[:].rearrange("p s (t m) -> p s m t", t=PACK),
+            ws_raw[:].rearrange("p (s m t) -> p s m t", s=2, t=PACK),
+        )
+
+        acc = [psum.tile([P, J], F32, name=f"acc{t}") for t in range(PACK)]
+        for t in range(PACK):
+            cols = slice(t * P, (t + 1) * P)
+            nc.tensor.matmul_mx(acc[t][:], w2_d[:, cols].bitcast(FP8X4), ws[:, 1, cols], xg_w[:].bitcast(FP4X4), xg_s[:], start=True, stop=False)
+
+        xi = tile([P, J, PACK], BF16, "xi", tag="ws_raw")
+        xq_w = tile([P, J], U32, "xq_w")
+        xq_s = tile([P, J], U8, "xq_s")
+        for h in range(2):
+            cols = slice(h * HALF, (h + 1) * HALF)
+            nc.vector.tensor_copy(
+                xi[:, cols, :].rearrange("p (c i) t -> p c t i", i=4), xb[:, :, cols].rearrange("p t (c i) -> p c t i", i=4)
+            )
+        for h in range(2):
+            cols = slice(h * HALF, (h + 1) * HALF)
+            nc.vector.quantize_mx(xq_w[:, cols].bitcast(FP8X4), xq_s[:, cols], xi[:, cols, :].rearrange("p j t -> p (j t)"))
+        for t in range(PACK):
+            cols = slice(t * P, (t + 1) * P)
+            nc.tensor.matmul_mx(acc[t][:], w_d[:, cols].bitcast(FP4X4), ws[:, 0, cols], xq_w[:].bitcast(FP8X4), xq_s[:], start=False, stop=True)
+
+        picked = tile([P, PACK, O], F32, "picked")
+        for t in range(PACK):
+            a_rows = tile([P, J], F32, f"a{t}")
+            nc.vector.tensor_copy(a_rows[:], acc[t][:])
+            nc.scalar.activation(picked[:, t, :], a_rows[:].indirect(l5[:]), COPY, scale=sa_c[:, t : t + 1])
+        capped = tile([P, PACK, O], F32, "capped")
+        for part in (slice(0, PACK - 1), slice(PACK - 1, PACK)):
+            nc.vector.tensor_tensor(capped[:, part, :], picked[:, part, :], upper[:, part, :], ALU.min)
+        hid = tile([P, O, PACK], BF16, "hid")
+        nc.vector.tensor_tensor(hid[:], capped[:].rearrange("p t o -> p o t"), lower[:].rearrange("p t o -> p o t"), ALU.max)
+        hq_w = tile([P, O], U32, "hq_w")
+        hq_s = tile([P, O], U8, "hq_s")
+        nc.vector.quantize_mx(hq_w[:].bitcast(FP8X4), hq_s[:], hid[:].rearrange("p o t -> p (o t)"))
+
+        for b in range(N // P):
+            cols = slice(b * P, (b + 1) * P)
+            res = psum.tile([P, O], F32, name=f"res{b}")
+            nc.tensor.matmul_mx(res[:], wb_w[:, cols].bitcast(FP8X4), wb_s[:, cols], hq_w[:].bitcast(FP8X4), hq_s[:], start=True, stop=True)
+            y = tile([P, O], F32, f"y{b}")
+            if b == 0:
+                nc.vector.tensor_copy(y[:], res[:])
+                nc.sync.dma_start(out[cols, :], y[:])
+            else:
+                nc.scalar.copy(y[:], res[:])
+                nc.scalar.dma_start(out[cols, :], y[:])

@@ -66,6 +66,10 @@ def tile_picked_codepage_plain_bank_codedbounds_one_plain_kernel(
         ga_c = load_column(nc.scalar, ga, "ga")
         l1 = load_list(offs, "l1")
         l2 = load_list(offs2, "l2")
+        warm_in = tile([P, 1], F32, "warm_in")
+        warm_out = tile([P, 1], F32, "warm_out")
+        nc.gpsimd.memset(warm_in[:], 0.0)
+        nc.scalar.activation(warm_out[:], warm_in[:], COPY)
         sl_c = load_column(nc.gpsimd, sl, "sl")
         sm_c = load_column(nc.gpsimd, sm, "sm")
         gb_c = load_column(nc.gpsimd, gb, "gb")

@@ -54,9 +54,9 @@ def tile_picked_codepage_plain_bank_codedbounds_one_plain_kernel(
                 queue.dma_start(dst[32 * q : 32 * q + 4, :].bitcast(I32), src[0, 4 * q : 4 * q + 4, :].bitcast(I32))
 
         xo_s = tile([P, M], U8, "xo_s")
-        ws_raw = tile([P, 2 * R], U8, "ws_raw")
+        ws_raw = [tile([P, R], U8, f"ws_raw{s}") for s in range(2)]
         wb_s = tile([P, N], U8, "wb_s")
-        for plane in (wb_s, xo_s, ws_raw):
+        for plane in (ws_raw[1], ws_raw[0], xo_s, wb_s):
             nc.vector.memset(plane[:].bitcast(I32), 0)
         page = [tile([P, U], F32, f"page{t}") for t in range(PACK)]
         for t in range(PACK):
@@ -74,7 +74,6 @@ def tile_picked_codepage_plain_bank_codedbounds_one_plain_kernel(
         sm_c = load_column(nc.gpsimd, sm, "sm")
         gb_c = load_column(nc.gpsimd, gb, "gb")
         sa_c = load_column(nc.gpsimd, sa, "sa")
-        load_scales(nc.gpsimd, wb_s, wb_scales)
         for t in range(1, 3):
             ta_rows.append(load_rows(ta, t, f"ta{t}"))
         w_raw = tile([P, R], U16, "w_raw")
@@ -89,23 +88,31 @@ def tile_picked_codepage_plain_bank_codedbounds_one_plain_kernel(
         xo_w = tile([P, M], U16, "xo_w")
         nc.sync.dma_start(xo_w[:].bitcast(I32), xo_words[0].bitcast(I32))
         l4 = load_list(offs4, "l4")
+        load_scales(nc.sync, ws_raw[1], w2_scales)
+        load_scales(nc.sync, ws_raw[0], w_scales)
         load_scales(nc.sync, xo_s, xo_scales)
-        load_scales(nc.sync, ws_raw[:, R:], w2_scales)
-        load_scales(nc.sync, ws_raw[:, :R], w_scales)
         tl_rows = tl_rows + [load_rows(tl, t, f"tl{t}") for t in range(2, PACK)]
         l5 = load_list(offs5, "l5")
         wb_w = tile([P, N], U32, "wb_w")
         nc.sync.dma_start(wb_w[:].bitcast(I32), wb_words[0].rearrange("p c r -> p (c r)").bitcast(I32))
+        load_scales(nc.sync, wb_s, wb_scales)
 
         for t in range(PACK):
             xcd = tile([P, J], F32, f"xcd{t}")
-            nc.scalar.activation(xcd[:], ta_rows[t][:].indirect(l1[:]), COPY, scale=ga_c[:, t : t + 1])
-            nc.vector.tensor_copy(page[t][:].indirect(l2[:]), xcd[:])
+            pieces = 2 if t == 0 else 1
+            for h in range(pieces):
+                cols = slice(h * J // pieces, (h + 1) * J // pieces)
+                lcols = slice(cols.start // 16, cols.stop // 16)
+                nc.scalar.activation(xcd[:, cols], ta_rows[t][:].indirect(l1[:, lcols]), COPY, scale=ga_c[:, t : t + 1])
+                nc.vector.tensor_copy(page[t][:].indirect(l2[:, lcols]), xcd[:, cols])
 
         w_d = tile([P, R], U16, "w_d")
         w2_d = tile([P, R], U32, "w2_d")
-        for dealt, raw in ((w_d, w_raw), (w2_d, w2_raw)):
-            nc.scalar.copy(dealt[:].rearrange("p (t m) -> p m t", t=PACK), raw[:].rearrange("p (m t) -> p m t", t=PACK))
+        for dealt, raw, run in ((w_d, w_raw, 8), (w2_d, w2_raw, 4)):
+            nc.scalar.copy(
+                dealt[:].rearrange("p (t c i) -> p c t i", t=PACK, i=run),
+                raw[:].rearrange("p (c i t) -> p c t i", t=PACK, i=run),
+            )
 
         upper = tile([P, PACK, O], F32, "upper")
         lower = tile([P, PACK, O], F32, "lower")
@@ -119,8 +126,6 @@ def tile_picked_codepage_plain_bank_codedbounds_one_plain_kernel(
         xb = tile([P, PACK, J], BF16, "xb", tag="tl1")
         for t in range(PACK):
             nc.scalar.activation(xb[:, t, :], page[t][:].indirect(l3[:]), COPY, scale=gb_c[:, t : t + 1])
-        for t in range(2, PACK):
-            fetch_bounds(t)
 
         xg_w = tile([P, J], U16, "xg_w")
         xg_s = tile([P, J], U8, "xg_s")
@@ -128,44 +133,64 @@ def tile_picked_codepage_plain_bank_codedbounds_one_plain_kernel(
         nc.vector.tensor_copy(xg_s[:], xo_s[:].indirect(l4[:]))
 
         ws = tile([P, 2, R], U8, "ws")
-        nc.vector.tensor_copy(
-            ws[:].rearrange("p s (t m) -> p s m t", t=PACK),
-            ws_raw[:].rearrange("p (s m t) -> p s m t", s=2, t=PACK),
-        )
-
-        acc = [psum.tile([P, J], F32, name=f"acc{t}") for t in range(PACK)]
-        for t in range(PACK):
-            cols = slice(t * P, (t + 1) * P)
-            nc.tensor.matmul_mx(acc[t][:], w2_d[:, cols].bitcast(FP8X4), ws[:, 1, cols], xg_w[:].bitcast(FP4X4), xg_s[:], start=True, stop=False)
-
-        xi = tile([P, J, PACK], BF16, "xi", tag="ws_raw")
-        xq_w = tile([P, J], U32, "xq_w")
-        xq_s = tile([P, J], U8, "xq_s")
-        for h in range(2):
-            cols = slice(h * HALF, (h + 1) * HALF)
-            nc.vector.tensor_copy(
-                xi[:, cols, :].rearrange("p (c i) t -> p c t i", i=4), xb[:, :, cols].rearrange("p t (c i) -> p c t i", i=4)
+        for s in (1, 0):
+            nc.gpsimd.tensor_copy(
+                ws[:, s, :].rearrange("p (t m) -> p t m", t=PACK), ws_raw[s][:].rearrange("p (m t) -> p t m", t=PACK)
             )
+
+        pieces = [(0, slice(0, HALF)), (0, slice(HALF, J))] + [(t, slice(0, J)) for t in range(1, PACK)]
+        acc = [psum.tile([P, js.stop - js.start], F32, name=f"acc{u}") for u, (t, js) in enumerate(pieces)]
+        for u, (t, js) in enumerate(pieces):
+            cols = slice(t * P, (t + 1) * P)
+            nc.tensor.matmul_mx(acc[u][:], w2_d[:, cols].bitcast(FP8X4), ws[:, 1, cols], xg_w[:, js].bitcast(FP4X4), xg_s[:, js], start=True, stop=False)
+
+        xi = [tile([P, HALF, PACK], BF16, "xi0"), tile([P, HALF, PACK], BF16, "xi1", tag="xo_s")]
+        xq_w = tile([P, J], U32, "xq_w", tag="tl1")
+        xq_s = tile([P, J], U8, "xq_s")
+        for h, copy in enumerate((nc.scalar.copy, nc.vector.tensor_copy)):
+            cols = slice(h * HALF, (h + 1) * HALF)
+            copy(xi[h][:].rearrange("p (c i) t -> p c t i", i=4), xb[:, :, cols].rearrange("p t (c i) -> p c t i", i=4))
+        for t in range(2, PACK):
+            fetch_bounds(t)
         for h in range(2):
             cols = slice(h * HALF, (h + 1) * HALF)
-            nc.vector.quantize_mx(xq_w[:, cols].bitcast(FP8X4), xq_s[:, cols], xi[:, cols, :].rearrange("p j t -> p (j t)"))
-        for t in range(PACK):
+            nc.vector.quantize_mx(xq_w[:, cols].bitcast(FP8X4), xq_s[:, cols], xi[h][:].rearrange("p j t -> p (j t)"))
+        for u, (t, js) in enumerate(pieces):
             cols = slice(t * P, (t + 1) * P)
-            nc.tensor.matmul_mx(acc[t][:], w_d[:, cols].bitcast(FP4X4), ws[:, 0, cols], xq_w[:].bitcast(FP8X4), xq_s[:], start=False, stop=True)
+            nc.tensor.matmul_mx(acc[u][:], w_d[:, cols].bitcast(FP4X4), ws[:, 0, cols], xq_w[:, js].bitcast(FP8X4), xq_s[:, js], start=False, stop=True)
 
         picked = tile([P, PACK, O], F32, "picked")
-        for t in range(PACK):
-            a_rows = tile([P, J], F32, f"a{t}")
-            nc.vector.tensor_copy(a_rows[:], acc[t][:])
-            nc.scalar.activation(picked[:, t, :], a_rows[:].indirect(l5[:]), COPY, scale=sa_c[:, t : t + 1])
+        a_rows = [tile([P, J], F32, f"a{t}") for t in range(PACK)]
+        halves = (slice(0, O // 2), slice(O // 2, O))
+        last = PACK - 1
+        for u, (t, js) in enumerate(pieces):
+            nc.vector.tensor_copy(a_rows[t][:, js], acc[u][:])
+            if js.stop == J:
+                for places in halves if t == last else (slice(0, O),):
+                    lcols = slice(places.start // 16, places.stop // 16)
+                    nc.scalar.activation(picked[:, t, places], a_rows[t][:].indirect(l5[:, lcols]), COPY, scale=sa_c[:, t : t + 1])
         capped = tile([P, PACK, O], F32, "capped")
-        for part in (slice(0, PACK - 1), slice(PACK - 1, PACK)):
-            nc.vector.tensor_tensor(capped[:, part, :], picked[:, part, :], upper[:, part, :], ALU.min)
         hid = tile([P, O, PACK], BF16, "hid")
-        nc.vector.tensor_tensor(hid[:], capped[:].rearrange("p t o -> p o t"), lower[:].rearrange("p t o -> p o t"), ALU.max)
+
+        def cap(ts, places):
+            nc.vector.tensor_tensor(capped[:, ts, places], picked[:, ts, places], upper[:, ts, places], ALU.min)
+
+        def floor(ts, places):
+            nc.vector.tensor_tensor(
+                hid[:, places, ts], capped[:, ts, places].rearrange("p t o -> p o t"), lower[:, ts, places].rearrange("p t o -> p o t"), ALU.max
+            )
+
+        cap(slice(0, 2), slice(0, O))
+        cap(slice(2, 3), slice(0, O))
+        floor(slice(0, 2), slice(0, O))
+        for places in halves:
+            cap(slice(3, 4), places)
+        for places in halves:
+            floor(slice(2, 4), places)
         hq_w = tile([P, O], U32, "hq_w")
         hq_s = tile([P, O], U8, "hq_s")
-        nc.vector.quantize_mx(hq_w[:].bitcast(FP8X4), hq_s[:], hid[:].rearrange("p o t -> p (o t)"))
+        for h, places in enumerate(halves):
+            nc.vector.quantize_mx(hq_w[:, places].bitcast(FP8X4), hq_s[:, places], hid[:, places, :].rearrange("p o t -> p (o t)"))
 
         for b in range(N // P):
             cols = slice(b * P, (b + 1) * P)

from contextlib import ExitStack

import concourse.mybir as mybir

K, J, R, T, U, Z, M, O, D, N = 512, 256, 512, 512, 512, 512, 1024, 128, 512, 256
FLOPS = 2 * (K * R * J + Z * R * J + R * N * O)

F32 = mybir.dt.float32
BF16 = mybir.dt.bfloat16
I32 = mybir.dt.int32
U32 = mybir.dt.uint32
U16 = mybir.dt.uint16
U8 = mybir.dt.uint8
FP8X4 = mybir.dt.float8_e4m3fn_x4
FP4X4 = mybir.dt.float4_e2m1fn_x4
COPY = mybir.ActivationFunctionType.Copy
ALU = mybir.AluOpType

P = 128
PACK = 4
QUADS = 4
HALF = J // 2


def tile_picked_codepage_plain_bank_codedbounds_one_plain_kernel(
    tc, ta, ga, gb, w_words, w_scales, xo_words, xo_scales, w2_words, w2_scales, tl, sa, sl, sm,
    wb_words, wb_scales, offs, offs2, offs3, offs4, offs5, offs6, offs7, out,
):
    nc = tc.nc
    with ExitStack() as ctx:
        keep = ctx.enter_context(tc.tile_pool(name="keep", bufs=1))
        psum = ctx.enter_context(tc.psum_pool(name="psum", bufs=1))

        def tile(shape, dtype, name, tag=None):
            return keep.tile(shape, dtype, name=name, tag=tag or name, align_bytes=64)

        def load_list(src, name):
            dst = tile(list(src.shape), U16, name)
            nc.sync.dma_start(dst[:], src)
            return dst

        def load_column(queue, src, name):
            dst = tile([P, PACK], F32, name)
            queue.dma_start(dst[:], src.rearrange("(p t) o -> p (t o)", t=PACK))
            return dst

        def load_rows(src, t, name):
            dst = tile([P, src.shape[1]], F32, name)
            nc.sync.dma_start(dst[:], src.rearrange("(p t) c -> t p c", t=PACK)[t])
            return dst

        def load_scales(queue, dst, src):
            for q in range(QUADS):
                queue.dma_start(dst[32 * q : 32 * q + 4, :].bitcast(I32), src[0, 4 * q : 4 * q + 4, :].bitcast(I32))

        xo_s = tile([P, M], U8, "xo_s")
        ws_raw = [tile([P, R], U8, f"ws_raw{s}") for s in range(2)]
        wb_s = tile([P, N], U8, "wb_s")
        for plane in (ws_raw[1], ws_raw[0], xo_s, wb_s):
            nc.vector.memset(plane[:].bitcast(I32), 0)
        page = [tile([P, U], F32, f"page{t}") for t in range(PACK)]
        for t in range(PACK):
            nc.vector.memset(page[t][:], 0.0)

        ta_rows = [load_rows(ta, 0, "ta0")]
        ga_c = load_column(nc.scalar, ga, "ga")
        l1 = load_list(offs, "l1")
        l2 = load_list(offs2, "l2")
        warm_in = tile([P, 1], F32, "warm_in")
        warm_out = tile([P, 1], F32, "warm_out")
        nc.gpsimd.memset(warm_in[:], 0.0)
        nc.scalar.activation(warm_out[:], warm_in[:], COPY)
        sl_c = load_column(nc.gpsimd, sl, "sl")
        sm_c = load_column(nc.gpsimd, sm, "sm")
        gb_c = load_column(nc.gpsimd, gb, "gb")
        sa_c = load_column(nc.gpsimd, sa, "sa")
        for t in range(1, 3):
            ta_rows.append(load_rows(ta, t, f"ta{t}"))
        w_raw = tile([P, R], U16, "w_raw")
        nc.sync.dma_start(w_raw[:].bitcast(I32), w_words[0].bitcast(I32))
        w2_raw = tile([P, R], U32, "w2_raw")
        nc.sync.dma_start(w2_raw[:].bitcast(I32), w2_words[0].rearrange("p c r -> p (c r)").bitcast(I32))
        ta_rows.append(load_rows(ta, 3, "ta3"))
        l6 = load_list(offs6, "l6")
        l7 = load_list(offs7, "l7")
        l3 = load_list(offs3, "l3")
        tl_rows = [load_rows(tl, t, f"tl{t}") for t in range(2)]
        xo_w = tile([P, M], U16, "xo_w")
        nc.sync.dma_start(xo_w[:].bitcast(I32), xo_words[0].bitcast(I32))
        l4 = load_list(offs4, "l4")
        load_scales(nc.sync, ws_raw[1], w2_scales)
        load_scales(nc.sync, ws_raw[0], w_scales)
        load_scales(nc.sync, xo_s, xo_scales)
        tl_rows = tl_rows + [load_rows(tl, t, f"tl{t}") for t in range(2, PACK)]
        l5 = load_list(offs5, "l5")
        wb_w = tile([P, N], U32, "wb_w")
        nc.sync.dma_start(wb_w[:].bitcast(I32), wb_words[0].rearrange("p c r -> p (c r)").bitcast(I32))
        load_scales(nc.sync, wb_s, wb_scales)

        for t in range(PACK):
            xcd = tile([P, J], F32, f"xcd{t}")
            pieces = 2 if t == 0 else 1
            for h in range(pieces):
                cols = slice(h * J // pieces, (h + 1) * J // pieces)
                lcols = slice(cols.start // 16, cols.stop // 16)
                nc.scalar.activation(xcd[:, cols], ta_rows[t][:].indirect(l1[:, lcols]), COPY, scale=ga_c[:, t : t + 1])
                nc.vector.tensor_copy(page[t][:].indirect(l2[:, lcols]), xcd[:, cols])

        w_d = tile([P, R], U16, "w_d")
        w2_d = tile([P, R], U32, "w2_d")
        for dealt, raw, run in ((w_d, w_raw, 8), (w2_d, w2_raw, 4)):
            nc.scalar.copy(
                dealt[:].rearrange("p (t c i) -> p c t i", t=PACK, i=run),
                raw[:].rearrange("p (c i t) -> p c t i", t=PACK, i=run),
            )

        upper = tile([P, PACK, O], F32, "upper")
        lower = tile([P, PACK, O], F32, "lower")

        def fetch_bounds(t):
            nc.scalar.activation(upper[:, t, :], tl_rows[t][:].indirect(l6[:]), COPY, scale=sl_c[:, t : t + 1])
            nc.scalar.activation(lower[:, t, :], tl_rows[t][:].indirect(l7[:]), COPY, scale=sm_c[:, t : t + 1])

        for t in range(2):
            fetch_bounds(t)
        xb = tile([P, PACK, J], BF16, "xb", tag="tl1")
        for t in range(PACK):
            nc.scalar.activation(xb[:, t, :], page[t][:].indirect(l3[:]), COPY, scale=gb_c[:, t : t + 1])

        xg_w = tile([P, J], U16, "xg_w")
        xg_s = tile([P, J], U8, "xg_s")
        nc.vector.tensor_copy(xg_w[:], xo_w[:].indirect(l4[:]))
        nc.vector.tensor_copy(xg_s[:], xo_s[:].indirect(l4[:]))

        ws = tile([P, 2, R], U8, "ws")
        for s in (1, 0):
            nc.gpsimd.tensor_copy(
                ws[:, s, :].rearrange("p (t m) -> p t m", t=PACK), ws_raw[s][:].rearrange("p (m t) -> p t m", t=PACK)
            )

        pieces = [(0, slice(0, HALF)), (0, slice(HALF, J))] + [(t, slice(0, J)) for t in range(1, PACK)]
        acc = [psum.tile([P, js.stop - js.start], F32, name=f"acc{u}") for u, (t, js) in enumerate(pieces)]
        for u, (t, js) in enumerate(pieces):
            cols = slice(t * P, (t + 1) * P)
            nc.tensor.matmul_mx(acc[u][:], w2_d[:, cols].bitcast(FP8X4), ws[:, 1, cols], xg_w[:, js].bitcast(FP4X4), xg_s[:, js], start=True, stop=False)

        xi = [tile([P, HALF, PACK], BF16, "xi0"), tile([P, HALF, PACK], BF16, "xi1", tag="xo_s")]
        xq_w = tile([P, J], U32, "xq_w", tag="tl1")
        xq_s = tile([P, J], U8, "xq_s")
        for h, copy in enumerate((nc.scalar.copy, nc.vector.tensor_copy)):
            cols = slice(h * HALF, (h + 1) * HALF)
            copy(xi[h][:].rearrange("p (c i) t -> p c t i", i=4), xb[:, :, cols].rearrange("p t (c i) -> p c t i", i=4))
        for t in range(2, PACK):
            fetch_bounds(t)
        for h in range(2):
            cols = slice(h * HALF, (h + 1) * HALF)
            nc.vector.quantize_mx(xq_w[:, cols].bitcast(FP8X4), xq_s[:, cols], xi[h][:].rearrange("p j t -> p (j t)"))
        for u, (t, js) in enumerate(pieces):
            cols = slice(t * P, (t + 1) * P)
            nc.tensor.matmul_mx(acc[u][:], w_d[:, cols].bitcast(FP4X4), ws[:, 0, cols], xq_w[:, js].bitcast(FP8X4), xq_s[:, js], start=False, stop=True)

        picked = tile([P, PACK, O], F32, "picked")
        a_rows = [tile([P, J], F32, f"a{t}") for t in range(PACK)]
        halves = (slice(0, O // 2), slice(O // 2, O))
        last = PACK - 1
        for u, (t, js) in enumerate(pieces):
            nc.vector.tensor_copy(a_rows[t][:, js], acc[u][:])
            if js.stop == J:
                for places in halves if t == last else (slice(0, O),):
                    lcols = slice(places.start // 16, places.stop // 16)
                    nc.scalar.activation(picked[:, t, places], a_rows[t][:].indirect(l5[:, lcols]), COPY, scale=sa_c[:, t : t + 1])
        capped = tile([P, PACK, O], F32, "capped")
        hid = tile([P, O, PACK], BF16, "hid")

        def cap(ts, places):
            nc.vector.tensor_tensor(capped[:, ts, places], picked[:, ts, places], upper[:, ts, places], ALU.min)

        def floor(ts, places):
            nc.vector.tensor_tensor(
                hid[:, places, ts], capped[:, ts, places].rearrange("p t o -> p o t"), lower[:, ts, places].rearrange("p t o -> p o t"), ALU.max
            )

        cap(slice(0, 2), slice(0, O))
        cap(slice(2, 3), slice(0, O))
        floor(slice(0, 2), slice(0, O))
        for places in halves:
            cap(slice(3, 4), places)
        for places in halves:
            floor(slice(2, 4), places)
        hq_w = tile([P, O], U32, "hq_w")
        hq_s = tile([P, O], U8, "hq_s")
        for h, places in enumerate(halves):
            nc.vector.quantize_mx(hq_w[:, places].bitcast(FP8X4), hq_s[:, places], hid[:, places, :].rearrange("p o t -> p (o t)"))

        for b in range(N // P):
            cols = slice(b * P, (b + 1) * P)
            res = psum.tile([P, O], F32, name=f"res{b}")
            nc.tensor.matmul_mx(res[:], wb_w[:, cols].bitcast(FP8X4), wb_s[:, cols], hq_w[:].bitcast(FP8X4), hq_s[:], start=True, stop=True)
            y = tile([P, O], F32, f"y{b}")
            if b == 0:
                nc.vector.tensor_copy(y[:], res[:])
                nc.sync.dma_start(out[cols, :], y[:])
            else:
                nc.scalar.copy(y[:], res[:])
                nc.scalar.dma_start(out[cols, :], y[:])
